import numpy as np
import ml_dtypes


def mxq(x, axis, fmt="e4m3"):
    dtype, down = {"e4m3": (ml_dtypes.float8_e4m3fn, 7), "e5m2": (ml_dtypes.float8_e5m2, 14)}[fmt]
    v = np.moveaxis(np.asarray(x, np.float32).astype(ml_dtypes.bfloat16).astype(np.float64), axis, -1)
    blocks = v.reshape(v.shape[:-1] + (-1, 32))
    amax = np.abs(blocks).max(-1, keepdims=True)
    byte = np.maximum(np.where(amax > 0, np.frexp(amax)[1] - 1 + 127, 0) - down, 1)
    scale = np.exp2(byte - 127.0)
    codes = (blocks / scale).astype(np.float32).astype(dtype).astype(np.float64)
    return np.moveaxis((codes * scale).reshape(v.shape), -1, axis)


WIDE = False


def mx_kscale(k):
    if not WIDE:
        return np.ones(k)
    levels = np.array([10, -10, 5, -5, 0])
    if k % 512:
        return np.exp2(np.random.permutation(np.resize(levels, k // 32))).repeat(32)
    a = np.empty((k // 512, 16))
    for p in range(k // 512):
        a[p, :8] = np.random.permutation(np.resize(levels, 8))
        for g in range(8):
            far = levels[np.abs(levels - a[p, g]) >= 10]
            a[p, g + 8] = far[np.random.randint(len(far))]
    return np.exp2(a.ravel()).repeat(32)


def f64(x):
    return np.asarray(x).astype(np.float64)


def striped(idx):
    return np.tile(idx.reshape(-1, 16).T, (8, 1)).astype(np.uint16)


def unstriped(offs):
    return offs[:16].T.reshape(-1).astype(np.int64)


def striped8(idx):
    return np.concatenate([x.reshape(-1, 16).T for x in idx]).astype(np.uint16)


def runs(offs, k):
    lists = np.stack([offs[16 * r : 16 * r + 16].T.reshape(-1) for r in range(8)]).astype(np.int64)
    return lists[np.arange(k) % 512 // 64]


def pack_weight(w):
    k, n = w.shape
    w = f64(np.asarray(w, np.float32).astype(ml_dtypes.bfloat16)).reshape(k // 32, 32, n)
    amax = np.abs(w).max(1)
    byte = np.clip(np.where(amax > 0, np.frexp(amax)[1] - 1 + 127 - 7, 1), 1, 254)
    scaled = (w * np.exp2(127.0 - byte)[:, None, :]).reshape(k, n).astype(np.float32)
    words = np.ascontiguousarray(scaled.reshape(k // 512, 128, 4, n).transpose(0, 1, 3, 2)).astype(ml_dtypes.float8_e4m3fn).view(np.uint8)
    return words, np.ascontiguousarray(byte.astype(np.uint8).reshape(k // 512, 16, n))


def unpack_weight(words, scales):
    g, p, n, _ = words.shape
    vals = np.ascontiguousarray(words).view(ml_dtypes.float8_e4m3fn).astype(np.float64) * np.repeat(np.exp2(scales.astype(np.float64) - 127.0), 8, axis=1)[..., None]
    return vals.transpose(0, 1, 3, 2).reshape(g * 512, n)


E2M1 = np.array([0.0, 0.5, 1.0, 1.5, 2.0, 3.0, 4.0, 6.0, -0.0, -0.5, -1.0, -1.5, -2.0, -3.0, -4.0, -6.0])


def pack_fp4(w):
    k, n = w.shape
    w = f64(np.asarray(w, np.float32).astype(ml_dtypes.bfloat16)).reshape(k // 32, 32, n)
    amax = np.abs(w).max(1)
    mant, ex = np.frexp(amax / 6.0)
    byte = np.clip(np.where(amax > 0, np.where(mant > 0.5, ex, ex - 1) + 127, 1), 1, 254)
    scaled = (w * np.exp2(127.0 - byte)[:, None, :]).reshape(k, n).astype(np.float32)
    c = np.ascontiguousarray(scaled.reshape(k // 512, 128, 4, n).transpose(0, 1, 3, 2)).astype(ml_dtypes.float4_e2m1fn).view(np.uint8) & 0xF
    words = (c[..., 0::2] | (c[..., 1::2] << 4)).reshape(k // 512, 128, 2 * n)
    return np.ascontiguousarray(words), np.ascontiguousarray(byte.astype(np.uint8).reshape(k // 512, 16, n))


def unpack_fp4(words, scales):
    g, _, n = scales.shape
    words = np.ascontiguousarray(words).reshape(g, 128, n, 2)
    nib = np.empty((g, 128, n, 4), np.uint8)
    nib[..., 0::2] = words & 0xF
    nib[..., 1::2] = words >> 4
    vals = E2M1[nib] * np.repeat(np.exp2(scales.astype(np.float64) - 127.0), 8, axis=1)[..., None]
    return vals.transpose(0, 1, 3, 2).reshape(g * 512, n)


def sigmoid(v):
    return 1.0 / (1.0 + np.exp(-np.maximum(v, -700.0)))

def planes(y):
    n, m = y.shape
    v = y.astype(np.float32).astype(ml_dtypes.bfloat16).astype(np.float64).reshape(n // 32, 32, m)
    top = np.abs(v).max(1)
    byte = np.clip(np.where(top > 0, np.frexp(top)[1] - 1 + 127 - 7, 1), 1, 254)
    codes = (v * np.exp2(127.0 - byte)[:, None, :]).reshape(n, m).astype(np.float32).astype(ml_dtypes.float8_e4m3fn).view(np.uint8)
    words = codes.reshape(n // 512, 128, 4, m).transpose(0, 1, 3, 2)
    return np.ascontiguousarray(words), np.ascontiguousarray(byte.astype(np.uint8).reshape(n // 512, 16, m))


K, T, S, H, C = 512, 2048, 512, 512, 512


def setup_inputs():
    n = np.random.standard_normal
    s = mx_kscale(K)[:, None]
    packed_xT = pack_weight(n((K, T)) * s)
    packed_w1 = pack_fp4(n((K, H)) / np.sqrt(K) / s)
    return {
        "x_words": packed_xT[0],
        "x_scales": packed_xT[1],
        "w1_words": packed_w1[0],
        "w1_scales": packed_w1[1],
        "gs": (np.random.uniform(0.5, 1.5, (K, 1)) / s).astype(np.float32),
        "gs2": (np.random.uniform(0.5, 1.5, (K, 1)) / s).astype(np.float32),
        "offs": striped(np.random.permutation(T)[:S]),
        "n1": striped(np.random.permutation(S)),
        "n2": striped(np.random.permutation(S)),
        "n3": striped8(np.stack([np.random.permutation(S) for _ in range(8)])),
        "n4": striped8(np.stack([np.random.permutation(S) for _ in range(8)])),
        "ca": striped(np.random.permutation(T)[:C]),
        "cb": striped(np.random.permutation(T)[:C]),
        "n5": striped8(np.stack([np.random.permutation(S) for _ in range(8)])),
        "n6": striped8(np.stack([np.random.permutation(S) for _ in range(8)])),
    }


def reference(x_words, x_scales, w1_words, w1_scales, gs, gs2, offs, n1, n2, n3, n4, ca, cb, n5, n6):
    x_ca = unpack_weight(x_words, x_scales)[:, unstriped(ca)]
    xq = unpack_weight(x_words, x_scales)[:, unstriped(offs)]
    y = unpack_fp4(w1_words, w1_scales).T @ xq
    st = y + 0.5 * y[:, unstriped(n1)]
    z = f64(gs) * (st - st[:, unstriped(n2)])
    a = 0.0625 * ((x_ca.T @ mxq(z, 0, "e4m3")))
    x_cb = unpack_weight(x_words, x_scales)[:, unstriped(cb)]
    pa = y[np.arange(H)[:, None], runs(n3, H)]
    pb = y[np.arange(H)[:, None], runs(n4, H)]
    z2 = f64(gs2) * (np.maximum(np.minimum(y, pa), np.minimum(np.maximum(y, pa), pb)))
    b = 0.0625 * ((x_cb.T @ mxq(z2, 0, "e4m3")))
    out_0 = (a + a[np.arange(C)[:, None], runs(n5, C)]) * (sigmoid(b + b[np.arange(C)[:, None], runs(n6, C)]))
    return (out_0,) + planes(out_0)

@@ -1,0 +1,272 @@
+from contextlib import ExitStack
+
+import concourse.mybir as mybir
+from concourse.masks import make_identity
+
+K, T, S, H, C = 512, 2048, 512, 512, 512
+FLOPS = 3 * 2 * 512 * 512 * 512
+
+F32 = mybir.dt.float32
+BF16 = mybir.dt.bfloat16
+I32 = mybir.dt.int32
+U32 = mybir.dt.uint32
+U16 = mybir.dt.uint16
+U8 = mybir.dt.uint8
+FP8X4 = mybir.dt.float8_e4m3fn_x4
+FP4X4 = mybir.dt.float4_e2m1fn_x4
+ALU = mybir.AluOpType
+ACT = mybir.ActivationFunctionType
+
+P = 128
+R = 4
+HALF = S // 2
+
+
+def tile_picked_twocdtriebhopmed_none_po_kernel(
+    tc, x_words, x_scales, w1_words, w1_scales, gs, gs2, offs, n1, n2, n3, n4, ca, cb, n5, n6, out_0, out_1, out_2
+):
+    nc = tc.nc
+    ADDER = nc.vector
+    with ExitStack() as ctx:
+        sb = ctx.enter_context(tc.tile_pool(name="sb", bufs=1))
+        ps = ctx.enter_context(tc.psum_pool(name="ps", bufs=1))
+
+        def tile(name, shape, dtype, tag=None):
+            return sb.tile(shape, dtype, name=name, tag=tag or name, align_bytes=64)
+
+        def load_list(name, src):
+            dst = tile("list_" + name, [P, S // 16], U16)
+            nc.sync.dma_start(dst[:], src)
+            return dst
+
+        def load_scales(name, src, width):
+            dst = tile(name, [P, width], U8)
+            for q in range(4):
+                rows = src[0, 4 * q : 4 * q + 4, :].bitcast(I32)
+                nc.sync.dma_start(
+                    dst[32 * q : 32 * (q + 1), :].bitcast(I32), rows.unsqueeze(0).broadcast_to([8, 4, width // 4])
+                )
+            return dst
+
+        l_offs = load_list("offs", offs)
+        l_cb = load_list("cb", cb)
+        xs = load_scales("xs", x_scales, T)
+        xw = tile("xw", [P, T], I32)
+        nc.sync.dma_start(xw[:], x_words[0].rearrange("p n t -> p (n t)").bitcast(I32))
+        w1w = tile("w1w", [P, 2 * H], U8)
+        nc.sync.dma_start(w1w[:].bitcast(I32), w1_words[0].bitcast(I32))
+        w1s = load_scales("w1s", w1_scales, H)
+        g2 = tile("g2", [P, R], F32)
+        nc.sync.dma_start(g2[:], gs2.rearrange("(p t) o -> p (t o)", t=R))
+        l_n3 = load_list("n3", n3)
+        l_n4 = load_list("n4", n4)
+        g1 = tile("g1", [P, R], F32)
+        nc.sync.dma_start(g1[:], gs.rearrange("(p t) o -> p (t o)", t=R))
+        l_ca = load_list("ca", ca)
+        l_n1 = load_list("n1", n1)
+        l_n2 = load_list("n2", n2)
+        l_n6 = load_list("n6", n6)
+        l_n5 = load_list("n5", n5)
+
+        def dealt(ap):
+            return ap.rearrange("p (t m) -> p m t", t=R)
+
+        def pick_scales(name, lst, view, tag=None):
+            dst = tile(name, [P, S], U8, tag)
+            nc.vector.tensor_copy(view(dst[:]), xs[:].indirect(lst[:]))
+            return dst
+
+        def pick_words(name, lst, view, tag=None):
+            dst = tile(name, [P, S], U32, tag)
+            nc.vector.tensor_copy(view(dst[:]), xw[:].bitcast(U32).indirect(lst[:]))
+            return dst
+
+        w1sd = tile("w1sd", [P, H], U8)
+        ident = tile("ident", [P, P], F32)
+        make_identity(nc, ident[:])
+        w1wd = tile("w1wd", [P, 2 * H], U8)
+        nc.scalar.copy(
+            w1wd[:].bitcast(U16).rearrange("p (t m) -> p t m", t=R),
+            w1w[:].bitcast(U16).rearrange("p (m t) -> p t m", t=R),
+        )
+
+        xq_s = pick_scales("xq_s", l_offs, lambda ap: ap)
+        cb_s = pick_scales("cb_s", l_cb, dealt)
+        xq_w = pick_words("xq_w", l_offs, lambda ap: ap)
+        nc.vector.tensor_copy(
+            w1sd[:].rearrange("p (t m) -> p t m", t=R), w1s[:].rearrange("p (m t) -> p t m", t=R)
+        )
+
+        y_ps = []
+        for t in range(R):
+            bank = ps.tile([P, S], F32, name="y%d" % t, tag="ya%d" % t)
+            nc.tensor.matmul_mx(
+                out=bank[:],
+                lhsT=w1wd[:, 2 * P * t : 2 * P * (t + 1)].bitcast(FP4X4),
+                lhsT_scale=w1sd[:, P * t : P * (t + 1)],
+                rhs=xq_w[:].bitcast(FP8X4),
+                rhs_scale=xq_s[:],
+                start=True,
+                stop=True,
+            )
+            y_ps.append(bank)
+
+        def cols(h):
+            return slice(HALF * h, HALF * (h + 1))
+
+        def lcols(h):
+            return slice(HALF // 16 * h, HALF // 16 * (h + 1))
+
+        def leave_psum(engine, dst, bank, scale):
+            if engine == "S":
+                nc.scalar.activation(dst, bank, ACT.Copy, scale=scale)
+            else:
+                nc.vector.tensor_scalar(dst, bank, scale, None, ALU.mult)
+
+        def fetch(engine, dst, window, lst, halves=(0, 1), scale=1.0):
+            for h in halves:
+                src = window.indirect(lst[:, lcols(h)])
+                if engine == "S":
+                    nc.scalar.activation(dst[:, cols(h)], src, ACT.Copy, scale=scale)
+                else:
+                    nc.vector.tensor_copy(dst[:, cols(h)], src)
+
+        def four(name):
+            return [tile("%s%d" % (name, t), [P, S], F32) for t in range(R)]
+
+        ya, yb, pa, pb, hi, hop1, bw, th_t, aw, ag = (
+            four(n) for n in ("ya", "yb", "pa", "pb", "hi", "hop1", "bw", "tht", "aw", "ag")
+        )
+        sa = tile("sa", [P, R, S], F32)
+        lo = tile("lo", [P, R, S], F32)
+        mid = tile("mid", [P, R, S], F32)
+        st = tile("st", [P, R, S], F32)
+        hop2 = tile("hop2", [P, R, S], F32)
+        res = tile("res", [P, R, S], F32)
+
+        def median_part(t):
+            nc.vector.tensor_tensor(hi[t][:], yb[t][:], pa[t][:], ALU.max)
+            nc.vector.tensor_tensor(lo[:, t, :], yb[t][:], pa[t][:], ALU.min)
+            nc.vector.tensor_tensor(mid[:, t, :], hi[t][:], pb[t][:], ALU.min)
+
+        def first_hop(t):
+            fetch("S", hop1[t], ya[t][:], l_n1, scale=0.5)
+
+        def first_sum(t):
+            ADDER.tensor_tensor(st[:, t, :], ya[t][:], hop1[t][:], ALU.add)
+
+        def by_pairs(src, h):
+            return src[:, :, cols(h)].rearrange("p t (c i) -> p c t i", i=2)
+
+        def woven(dst):
+            return dst[:].rearrange("p (c i t) -> p c t i", i=2, t=R)
+
+        def quantise(name, make):
+            words = tile(name + "_w", [P, S], U32)
+            scales = tile(name + "_s", [P, S], U8)
+            rounded = [tile("%s_r%d" % (name, h), [P, R * HALF], BF16) for h in range(2)]
+            for h in range(2):
+                make(woven(rounded[h]), h)
+            for h in range(2):
+                nc.vector.quantize_mx(words[:, cols(h)].bitcast(FP8X4), scales[:, cols(h)], rounded[h][:])
+            return words, scales
+
+        def score(tag, name, lhs_w, lhs_s, rhs_w, rhs_s):
+            banks = [ps.tile([P, S], F32, name="%s%d" % (name, t), tag="%s%d" % (tag, t)) for t in range(R)]
+            for t in range(R):
+                for h in range(2):
+                    nc.tensor.matmul_mx(
+                        out=banks[t][:, cols(h)],
+                        lhsT=lhs_w[:, P * t : P * (t + 1)].bitcast(FP8X4),
+                        lhsT_scale=lhs_s[:, P * t : P * (t + 1)],
+                        rhs=rhs_w[:, cols(h)].bitcast(FP8X4),
+                        rhs_scale=rhs_s[:, cols(h)],
+                        start=True,
+                        stop=True,
+                    )
+            return banks
+
+        N6, EA = "VVVV", "VVVV"
+        for t in range(R):
+            leave_psum("S" if t == 0 else "V", yb[t][:], y_ps[t][:], g2[:, t : t + 1])
+            fetch("S", pa[t], yb[t][:], l_n3)
+            fetch("S", pb[t], yb[t][:], l_n4)
+        cb_w = pick_words("cb_w", l_cb, dealt, "xq_w")
+        median_part(0)
+        ca_s = pick_scales("ca_s", l_ca, dealt, "xq_s")
+        leave_psum("V", ya[0][:], y_ps[0][:], g1[:, 0:1])
+        for t in range(1, R):
+            leave_psum("V", ya[t][:], y_ps[t][:], g1[:, t : t + 1])
+            median_part(t)
+        for t in range(R):
+            first_hop(t)
+        z2_w, z2_s = quantise(
+            "z2", lambda dst, h: nc.vector.tensor_tensor(dst, by_pairs(lo, h), by_pairs(mid, h), ALU.max)
+        )
+        b_ps = score("b", "b", cb_w, cb_s, z2_w, z2_s)
+        for t in range(R):
+            first_sum(t)
+            if t < 3:
+                fetch("S", hop2[:, t, :], st[:, t, :], l_n2)
+        ca_w = pick_words("ca_w", l_ca, dealt, "xq_w")
+        fetch("V", hop2[:, 3, :], st[:, 3, :], l_n2)
+        z_w, z_s = quantise(
+            "z", lambda dst, h: nc.vector.tensor_tensor(dst, by_pairs(st, h), by_pairs(hop2, h), ALU.subtract)
+        )
+        a_ps = score("ya", "a", ca_w, ca_s, z_w, z_s)
+        bg = [tile("bg0", [P, S], F32), tile("bg1", [P, S], F32)]
+        bg = bg + [tile("bg2", [P, S], F32, "z_r0"), tile("bg3", [P, S], F32, "z_r1")]
+        for pair in range(2):
+            for t in (2 * pair, 2 * pair + 1):
+                leave_psum("S", bw[t][:], b_ps[t][:], 0.0625 * 0.5)
+            for t in (2 * pair, 2 * pair + 1):
+                fetch("S", bg[t], bw[t][:], l_n6, halves=(0,))
+        for t in range(R):
+            leave_psum(EA[t], aw[t][:], a_ps[t][:], 0.0625 * 0.5)
+            fetch(N6[t], bg[t], bw[t][:], l_n6, halves=(1,))
+        gates = []
+        for h in range(2):
+            for pair in range(2):
+                u = 2 * h + pair
+                total = ps.tile([P, S], F32, name="sum%d" % u, tag="b%d" % u)
+                blocks = [(2 * pair + j // 2, HALF * h + P * (j % 2), slice(P * j, P * (j + 1))) for j in range(4)]
+                for j, (t, c0, blk) in enumerate(blocks):
+                    nc.tensor.matmul(
+                        total[:, blk], bw[t][:, c0 : c0 + P], ident[:], start=j == 0, stop=False, is_transpose=True
+                    )
+                for j, (t, c0, blk) in enumerate(blocks):
+                    nc.tensor.matmul(
+                        total[:, blk], bg[t][:, c0 : c0 + P], ident[:], start=False, stop=j == 3, is_transpose=True
+                    )
+                nc.scalar.activation(th_t[u][:], total[:], ACT.Tanh)
+                back = ps.tile([P, S], F32, name="th%d" % u, tag="b%d" % u)
+                for j, (t, c0, blk) in enumerate(blocks):
+                    nc.tensor.transpose(back[:, blk], th_t[u][:, blk], ident[:])
+                gates.append(back)
+
+        out_rows = out_0.rearrange("(p t) n -> p t n", t=R)
+        words_out = out_1[0].rearrange("p n t -> p (n t)").bitcast(I32)
+        o_w = tile("o_w", [P, S], U32)
+        o_s = tile("o_s", [P, S], U8)
+        for h in range(2):
+            for pair in range(2):
+                rows = slice(2 * pair, 2 * pair + 2)
+                for t in (2 * pair, 2 * pair + 1):
+                    fetch("S", ag[t], aw[t][:], l_n5, halves=(h,))
+                    ADDER.tensor_tensor(sa[:, t, cols(h)], aw[t][:, cols(h)], ag[t][:, cols(h)], ALU.add)
+                nc.vector.scalar_tensor_tensor(
+                    res[:, rows, cols(h)],
+                    gates[2 * h + pair][:].rearrange("p (t c) -> p t c", t=2),
+                    1.0,
+                    sa[:, rows, cols(h)],
+                    ALU.add,
+                    ALU.mult,
+                )
+                nc.sync.dma_start(out_rows[:, rows, cols(h)], res[:, rows, cols(h)])
+            rounded = tile("o_r%d" % h, [P, R * HALF], BF16)
+            nc.vector.tensor_copy(woven(rounded), by_pairs(res, h))
+            nc.vector.quantize_mx(o_w[:, cols(h)].bitcast(FP8X4), o_s[:, cols(h)], rounded[:])
+            nc.sync.dma_start(words_out[:, cols(h)], o_w[:, cols(h)].bitcast(I32))
+        for q in range(4):
+            engine = nc.scalar if q % 2 else nc.sync
+            engine.dma_start(out_2[0, 4 * q : 4 * q + 4, :].bitcast(I32), o_s[32 * q : 32 * q + 4, :].bitcast(I32))

@@ -1,10 +1,9 @@
 from contextlib import ExitStack
 
 import concourse.mybir as mybir
-from concourse.masks import make_identity
 
 K, T, S, H, C = 512, 2048, 512, 512, 512
-FLOPS = 3 * 2 * 512 * 512 * 512
+FLOPS = 2 * K * H * S + 2 * (2 * H * C * S)
 
 F32 = mybir.dt.float32
 BF16 = mybir.dt.bfloat16
@@ -20,19 +19,32 @@ ACT = mybir.ActivationFunctionType
 P = 128
 R = 4
 HALF = S // 2
+SCORE_FACTOR = 0.0625 * 0.5
+
+SCALED_ON_GPSIMD = 2
+N3_ON_VECTOR = 3
+A_ON_VECTOR = 1
+N6_ON_VECTOR = 3
+ROUNDED_ON_SCALAR = 3
+EARLY_MIDDLES = 1
 
 
 def tile_picked_twocdtriebhopmed_none_po_kernel(
     tc, x_words, x_scales, w1_words, w1_scales, gs, gs2, offs, n1, n2, n3, n4, ca, cb, n5, n6, out_0, out_1, out_2
 ):
     nc = tc.nc
-    ADDER = nc.vector
     with ExitStack() as ctx:
-        sb = ctx.enter_context(tc.tile_pool(name="sb", bufs=1))
-        ps = ctx.enter_context(tc.psum_pool(name="ps", bufs=1))
+        sbuf = ctx.enter_context(tc.tile_pool(name="sbuf", bufs=1))
+        psum = ctx.enter_context(tc.psum_pool(name="psum", bufs=1))
 
-        def tile(name, shape, dtype, tag=None):
-            return sb.tile(shape, dtype, name=name, tag=tag or name, align_bytes=64)
+        def tile(name, shape, dtype, after=None):
+            return sbuf.tile(shape, dtype, name=name, tag=after or name, align_bytes=64)
+
+        def planes(name):
+            return [tile("%s%d" % (name, t), [P, S], F32) for t in range(R)]
+
+        def cols(h):
+            return slice(HALF * h, HALF * (h + 1))
 
         def load_list(name, src):
             dst = tile("list_" + name, [P, S // 16], U16)
@@ -48,225 +60,226 @@ def tile_picked_twocdtriebhopmed_none_po_kernel(
                 )
             return dst
 
+        def load_factors(name, src):
+            dst = tile(name, [P, R], F32)
+            nc.sync.dma_start(dst[:], src.rearrange("(p t) o -> p (t o)", t=R))
+            return dst
+
         l_offs = load_list("offs", offs)
-        l_cb = load_list("cb", cb)
+        l_ca = load_list("ca", ca)
         xs = load_scales("xs", x_scales, T)
         xw = tile("xw", [P, T], I32)
         nc.sync.dma_start(xw[:], x_words[0].rearrange("p n t -> p (n t)").bitcast(I32))
         w1w = tile("w1w", [P, 2 * H], U8)
         nc.sync.dma_start(w1w[:].bitcast(I32), w1_words[0].bitcast(I32))
         w1s = load_scales("w1s", w1_scales, H)
-        g2 = tile("g2", [P, R], F32)
-        nc.sync.dma_start(g2[:], gs2.rearrange("(p t) o -> p (t o)", t=R))
-        l_n3 = load_list("n3", n3)
-        l_n4 = load_list("n4", n4)
-        g1 = tile("g1", [P, R], F32)
-        nc.sync.dma_start(g1[:], gs.rearrange("(p t) o -> p (t o)", t=R))
-        l_ca = load_list("ca", ca)
+        g1 = load_factors("g1", gs)
         l_n1 = load_list("n1", n1)
+        g2 = load_factors("g2", gs2)
         l_n2 = load_list("n2", n2)
-        l_n6 = load_list("n6", n6)
+        l_cb = load_list("cb", cb)
+        l_n4 = load_list("n4", n4)
+        l_n3 = load_list("n3", n3)
         l_n5 = load_list("n5", n5)
+        l_n6 = load_list("n6", n6)
 
         def dealt(ap):
             return ap.rearrange("p (t m) -> p m t", t=R)
 
-        def pick_scales(name, lst, view, tag=None):
-            dst = tile(name, [P, S], U8, tag)
-            nc.vector.tensor_copy(view(dst[:]), xs[:].indirect(lst[:]))
+        def pick_dealt_scales(name, lst, after=None):
+            dst = tile(name, [P, C], U8, after)
+            nc.vector.tensor_copy(dealt(dst[:]), xs[:].indirect(lst[:]))
             return dst
 
-        def pick_words(name, lst, view, tag=None):
-            dst = tile(name, [P, S], U32, tag)
-            nc.vector.tensor_copy(view(dst[:]), xw[:].bitcast(U32).indirect(lst[:]))
+        def pick_dealt_words(name, lst, after):
+            dst = tile(name, [P, C], U32, after)
+            nc.vector.tensor_copy(dealt(dst[:]), xw[:].bitcast(U32).indirect(lst[:]))
             return dst
 
-        w1sd = tile("w1sd", [P, H], U8)
-        ident = tile("ident", [P, P], F32)
-        make_identity(nc, ident[:])
-        w1wd = tile("w1wd", [P, 2 * H], U8)
+        w1w_dealt = tile("w1w_dealt", [P, 2 * H], U8)
         nc.scalar.copy(
-            w1wd[:].bitcast(U16).rearrange("p (t m) -> p t m", t=R),
+            w1w_dealt[:].bitcast(U16).rearrange("p (t m) -> p t m", t=R),
             w1w[:].bitcast(U16).rearrange("p (m t) -> p t m", t=R),
         )
-
-        xq_s = pick_scales("xq_s", l_offs, lambda ap: ap)
-        cb_s = pick_scales("cb_s", l_cb, dealt)
-        xq_w = pick_words("xq_w", l_offs, lambda ap: ap)
+        xq_s = tile("xq_s", [P, S], U8)
+        nc.vector.tensor_copy(xq_s[:], xs[:].indirect(l_offs[:]))
+        ca_s = pick_dealt_scales("ca_s", l_ca)
+        xq_w = tile("xq_w", [P, S], U32)
+        nc.vector.tensor_copy(xq_w[:], xw[:].bitcast(U32).indirect(l_offs[:]))
+        w1s_dealt = tile("w1s_dealt", [P, H], U8)
         nc.vector.tensor_copy(
-            w1sd[:].rearrange("p (t m) -> p t m", t=R), w1s[:].rearrange("p (m t) -> p t m", t=R)
+            w1s_dealt[:].rearrange("p (t m) -> p t m", t=R), w1s[:].rearrange("p (m t) -> p t m", t=R)
         )
 
-        y_ps = []
+        y_ps = [psum.tile([P, S], F32, name="y%d" % t, tag="y_then_b%d" % t) for t in range(R)]
         for t in range(R):
-            bank = ps.tile([P, S], F32, name="y%d" % t, tag="ya%d" % t)
             nc.tensor.matmul_mx(
-                out=bank[:],
-                lhsT=w1wd[:, 2 * P * t : 2 * P * (t + 1)].bitcast(FP4X4),
-                lhsT_scale=w1sd[:, P * t : P * (t + 1)],
+                out=y_ps[t][:],
+                lhsT=w1w_dealt[:, 2 * P * t : 2 * P * (t + 1)].bitcast(FP4X4),
+                lhsT_scale=w1s_dealt[:, P * t : P * (t + 1)],
                 rhs=xq_w[:].bitcast(FP8X4),
                 rhs_scale=xq_s[:],
                 start=True,
                 stop=True,
             )
-            y_ps.append(bank)
 
-        def cols(h):
-            return slice(HALF * h, HALF * (h + 1))
-
-        def lcols(h):
-            return slice(HALF // 16 * h, HALF // 16 * (h + 1))
-
-        def leave_psum(engine, dst, bank, scale):
-            if engine == "S":
-                nc.scalar.activation(dst, bank, ACT.Copy, scale=scale)
+        def leave_psum(on_vector, dst, bank, factor):
+            if on_vector:
+                nc.vector.tensor_scalar(dst, bank, factor, None, ALU.mult)
             else:
-                nc.vector.tensor_scalar(dst, bank, scale, None, ALU.mult)
+                nc.scalar.activation(dst, bank, ACT.Copy, scale=factor)
 
-        def fetch(engine, dst, window, lst, halves=(0, 1), scale=1.0):
-            for h in halves:
-                src = window.indirect(lst[:, lcols(h)])
-                if engine == "S":
-                    nc.scalar.activation(dst[:, cols(h)], src, ACT.Copy, scale=scale)
-                else:
-                    nc.vector.tensor_copy(dst[:, cols(h)], src)
+        def fetch_half(on_vector, dst, window, lst, h, factor=1.0):
+            src = window.indirect(lst[:, HALF // 16 * h : HALF // 16 * (h + 1)])
+            if on_vector:
+                nc.vector.tensor_copy(dst[:, cols(h)], src)
+            else:
+                nc.scalar.activation(dst[:, cols(h)], src, ACT.Copy, scale=factor)
 
-        def four(name):
-            return [tile("%s%d" % (name, t), [P, S], F32) for t in range(R)]
+        def fetch(on_vector, dst, window, lst, factor=1.0):
+            for h in range(2):
+                fetch_half(on_vector, dst, window, lst, h, factor)
 
-        ya, yb, pa, pb, hi, hop1, bw, th_t, aw, ag = (
-            four(n) for n in ("ya", "yb", "pa", "pb", "hi", "hop1", "bw", "tht", "aw", "ag")
-        )
-        sa = tile("sa", [P, R, S], F32)
-        lo = tile("lo", [P, R, S], F32)
-        mid = tile("mid", [P, R, S], F32)
-        st = tile("st", [P, R, S], F32)
-        hop2 = tile("hop2", [P, R, S], F32)
-        res = tile("res", [P, R, S], F32)
+        def scale_on_gpsimd(dst, src, factor):
+            nc.gpsimd.tensor_scalar(dst, src, factor, 0.0, ALU.mult, ALU.add)
 
-        def median_part(t):
-            nc.vector.tensor_tensor(hi[t][:], yb[t][:], pa[t][:], ALU.max)
-            nc.vector.tensor_tensor(lo[:, t, :], yb[t][:], pa[t][:], ALU.min)
-            nc.vector.tensor_tensor(mid[:, t, :], hi[t][:], pb[t][:], ALU.min)
-
-        def first_hop(t):
-            fetch("S", hop1[t], ya[t][:], l_n1, scale=0.5)
-
-        def first_sum(t):
-            ADDER.tensor_tensor(st[:, t, :], ya[t][:], hop1[t][:], ALU.add)
-
-        def by_pairs(src, h):
-            return src[:, :, cols(h)].rearrange("p t (c i) -> p c t i", i=2)
+        def in_pairs(src):
+            return src.rearrange("p t (c i) -> p c t i", i=2)
 
         def woven(dst):
             return dst[:].rearrange("p (c i t) -> p c t i", i=2, t=R)
 
-        def quantise(name, make):
+        def quantise(name, left, right, op):
             words = tile(name + "_w", [P, S], U32)
             scales = tile(name + "_s", [P, S], U8)
-            rounded = [tile("%s_r%d" % (name, h), [P, R * HALF], BF16) for h in range(2)]
             for h in range(2):
-                make(woven(rounded[h]), h)
-            for h in range(2):
-                nc.vector.quantize_mx(words[:, cols(h)].bitcast(FP8X4), scales[:, cols(h)], rounded[h][:])
+                rounded = tile("%s_rounded%d" % (name, h), [P, R * HALF], BF16)
+                nc.vector.tensor_tensor(woven(rounded), in_pairs(left[:, :, cols(h)]), in_pairs(right[:, :, cols(h)]), op)
+                nc.vector.quantize_mx(words[:, cols(h)].bitcast(FP8X4), scales[:, cols(h)], rounded[:])
             return words, scales
 
-        def score(tag, name, lhs_w, lhs_s, rhs_w, rhs_s):
-            banks = [ps.tile([P, S], F32, name="%s%d" % (name, t), tag="%s%d" % (tag, t)) for t in range(R)]
-            for t in range(R):
-                for h in range(2):
-                    nc.tensor.matmul_mx(
-                        out=banks[t][:, cols(h)],
-                        lhsT=lhs_w[:, P * t : P * (t + 1)].bitcast(FP8X4),
-                        lhsT_scale=lhs_s[:, P * t : P * (t + 1)],
-                        rhs=rhs_w[:, cols(h)].bitcast(FP8X4),
-                        rhs_scale=rhs_s[:, cols(h)],
-                        start=True,
-                        stop=True,
-                    )
-            return banks
+        def score(out, t, h, picked_w, picked_s, words, scales):
+            nc.tensor.matmul_mx(
+                out=out,
+                lhsT=picked_w[:, P * t : P * (t + 1)].bitcast(FP8X4),
+                lhsT_scale=picked_s[:, P * t : P * (t + 1)],
+                rhs=words[:, cols(h)].bitcast(FP8X4),
+                rhs_scale=scales[:, cols(h)],
+                start=True,
+                stop=True,
+            )
 
-        N6, EA = "VVVV", "VVVV"
+        ya, yb, hop1, pa, pb, hi = (planes(n) for n in ("ya", "yb", "hop1_", "pa", "pb", "hi"))
+        unscaled_st = tile("unscaled_st", [P, R, S], F32)
+        st = tile("st", [P, R, S], F32)
+        hop2 = tile("hop2", [P, R, S], F32)
+        lo = tile("lo", [P, R, S], F32)
         for t in range(R):
-            leave_psum("S" if t == 0 else "V", yb[t][:], y_ps[t][:], g2[:, t : t + 1])
-            fetch("S", pa[t], yb[t][:], l_n3)
-            fetch("S", pb[t], yb[t][:], l_n4)
-        cb_w = pick_words("cb_w", l_cb, dealt, "xq_w")
-        median_part(0)
-        ca_s = pick_scales("ca_s", l_ca, dealt, "xq_s")
-        leave_psum("V", ya[0][:], y_ps[0][:], g1[:, 0:1])
-        for t in range(1, R):
-            leave_psum("V", ya[t][:], y_ps[t][:], g1[:, t : t + 1])
-            median_part(t)
+            leave_psum(t > 0, ya[t][:], y_ps[t][:], 1.0 if t < SCALED_ON_GPSIMD else g1[:, t : t + 1])
+            fetch(False, hop1[t], ya[t][:], l_n1, 0.5)
+        for t in range(SCALED_ON_GPSIMD):
+            scale_on_gpsimd(yb[t][:], ya[t][:], g2[:, t : t + 1])
         for t in range(R):
-            first_hop(t)
-        z2_w, z2_s = quantise(
-            "z2", lambda dst, h: nc.vector.tensor_tensor(dst, by_pairs(lo, h), by_pairs(mid, h), ALU.max)
-        )
-        b_ps = score("b", "b", cb_w, cb_s, z2_w, z2_s)
+            if t < SCALED_ON_GPSIMD:
+                nc.gpsimd.tensor_tensor(unscaled_st[:, t, :], ya[t][:], hop1[t][:], ALU.add)
+                scale_on_gpsimd(st[:, t, :], unscaled_st[:, t, :], g1[:, t : t + 1])
+            else:
+                nc.gpsimd.tensor_tensor(st[:, t, :], ya[t][:], hop1[t][:], ALU.add)
+        ca_w = pick_dealt_words("ca_w", l_ca, "w1s")
+        cb_s = pick_dealt_scales("cb_s", l_cb, "xq_s")
+        for t in range(SCALED_ON_GPSIMD, R):
+            leave_psum(t < N3_ON_VECTOR, yb[t][:], y_ps[t][:], g2[:, t : t + 1])
+        cb_w = pick_dealt_words("cb_w", l_cb, "xq_w")
         for t in range(R):
-            first_sum(t)
-            if t < 3:
-                fetch("S", hop2[:, t, :], st[:, t, :], l_n2)
-        ca_w = pick_words("ca_w", l_ca, dealt, "xq_w")
-        fetch("V", hop2[:, 3, :], st[:, 3, :], l_n2)
-        z_w, z_s = quantise(
-            "z", lambda dst, h: nc.vector.tensor_tensor(dst, by_pairs(st, h), by_pairs(hop2, h), ALU.subtract)
-        )
-        a_ps = score("ya", "a", ca_w, ca_s, z_w, z_s)
-        bg = [tile("bg0", [P, S], F32), tile("bg1", [P, S], F32)]
-        bg = bg + [tile("bg2", [P, S], F32, "z_r0"), tile("bg3", [P, S], F32, "z_r1")]
-        for pair in range(2):
-            for t in (2 * pair, 2 * pair + 1):
-                leave_psum("S", bw[t][:], b_ps[t][:], 0.0625 * 0.5)
-            for t in (2 * pair, 2 * pair + 1):
-                fetch("S", bg[t], bw[t][:], l_n6, halves=(0,))
+            fetch(False, hop2[:, t, :], st[:, t, :], l_n2)
+
         for t in range(R):
-            leave_psum(EA[t], aw[t][:], a_ps[t][:], 0.0625 * 0.5)
-            fetch(N6[t], bg[t], bw[t][:], l_n6, halves=(1,))
-        gates = []
+            if t >= N3_ON_VECTOR:
+                fetch(False, pa[t], yb[t][:], l_n3)
+            fetch(False, pb[t], yb[t][:], l_n4)
+        for t in range(N3_ON_VECTOR):
+            fetch(True, pa[t], yb[t][:], l_n3)
+        mid = tile("mid", [P, R, S], F32, "unscaled_st")
+
+        def bounds(t):
+            nc.vector.scalar_tensor_tensor(hi[t][:], y_ps[t][:], g2[:, t : t + 1], pa[t][:], ALU.mult, ALU.max)
+            nc.vector.scalar_tensor_tensor(lo[:, t, :], y_ps[t][:], g2[:, t : t + 1], pa[t][:], ALU.mult, ALU.min)
+
+        def middle(t):
+            nc.vector.tensor_tensor(mid[:, t, :], hi[t][:], pb[t][:], ALU.min)
+
+        for t in range(N3_ON_VECTOR):
+            bounds(t)
+        for t in range(EARLY_MIDDLES):
+            middle(t)
+
+        z_w, z_s = quantise("z", st, hop2, ALU.subtract)
+        a_ps = [psum.tile([P, S], F32, name="a%d" % t) for t in range(R)]
+        for t in range(R):
+            for h in range(2):
+                score(a_ps[t][:, cols(h)], t, h, ca_w, ca_s, z_w, z_s)
+        aw, ag, bw = (planes(n) for n in ("aw", "ag", "bw"))
+        for t in range(A_ON_VECTOR):
+            leave_psum(True, aw[t][:], a_ps[t][:], SCORE_FACTOR)
+        for t in range(R):
+            if t >= N3_ON_VECTOR:
+                bounds(t)
+            if t >= EARLY_MIDDLES:
+                middle(t)
+        z2_w, z2_s = quantise("z2", lo, mid, ALU.max)
+        for t in range(A_ON_VECTOR, R):
+            leave_psum(False, aw[t][:], a_ps[t][:], SCORE_FACTOR)
+
+        b_ps = [psum.tile([P, 2, HALF], F32, name="b%d" % u, tag="y_then_b%d" % u) for u in range(R)]
         for h in range(2):
-            for pair in range(2):
-                u = 2 * h + pair
-                total = ps.tile([P, S], F32, name="sum%d" % u, tag="b%d" % u)
-                blocks = [(2 * pair + j // 2, HALF * h + P * (j % 2), slice(P * j, P * (j + 1))) for j in range(4)]
-                for j, (t, c0, blk) in enumerate(blocks):
-                    nc.tensor.matmul(
-                        total[:, blk], bw[t][:, c0 : c0 + P], ident[:], start=j == 0, stop=False, is_transpose=True
-                    )
-                for j, (t, c0, blk) in enumerate(blocks):
-                    nc.tensor.matmul(
-                        total[:, blk], bg[t][:, c0 : c0 + P], ident[:], start=False, stop=j == 3, is_transpose=True
-                    )
-                nc.scalar.activation(th_t[u][:], total[:], ACT.Tanh)
-                back = ps.tile([P, S], F32, name="th%d" % u, tag="b%d" % u)
-                for j, (t, c0, blk) in enumerate(blocks):
-                    nc.tensor.transpose(back[:, blk], th_t[u][:, blk], ident[:])
-                gates.append(back)
+            for t in range(R):
+                score(b_ps[2 * h + t // 2][:, t % 2, :], t, h, cb_w, cb_s, z2_w, z2_s)
+        for h in range(2):
+            for t in range(R):
+                leave_psum(True, bw[t][:, cols(h)], b_ps[2 * h + t // 2][:, t % 2, :], SCORE_FACTOR)
+        for t in range(R):
+            fetch(False, ag[t], aw[t][:], l_n5)
 
-        out_rows = out_0.rearrange("(p t) n -> p t n", t=R)
-        words_out = out_1[0].rearrange("p n t -> p (n t)").bitcast(I32)
-        o_w = tile("o_w", [P, S], U32)
-        o_s = tile("o_s", [P, S], U8)
+        a_sum = tile("a_sum", [P, R, S], F32, "z2_rounded1")
+        for h in range(2):
+            for t in range(R):
+                nc.gpsimd.tensor_tensor(a_sum[:, t, cols(h)], aw[t][:, cols(h)], ag[t][:, cols(h)], ALU.add)
+
+        bg = tile("bg", [P, R, S], F32)
+        b_sum = tile("b_sum", [P, R, S], F32)
+        th = tile("th", [P, R, S], F32)
+        res = tile("res", [P, R, S], F32)
         for h in range(2):
             for pair in range(2):
                 rows = slice(2 * pair, 2 * pair + 2)
                 for t in (2 * pair, 2 * pair + 1):
-                    fetch("S", ag[t], aw[t][:], l_n5, halves=(h,))
-                    ADDER.tensor_tensor(sa[:, t, cols(h)], aw[t][:, cols(h)], ag[t][:, cols(h)], ALU.add)
+                    fetch_half(R * h + t < N6_ON_VECTOR, bg[:, t, :], bw[t][:], l_n6, h)
                 nc.vector.scalar_tensor_tensor(
-                    res[:, rows, cols(h)],
-                    gates[2 * h + pair][:].rearrange("p (t c) -> p t c", t=2),
-                    1.0,
-                    sa[:, rows, cols(h)],
-                    ALU.add,
-                    ALU.mult,
+                    b_sum[:, rows, cols(h)], b_ps[2 * h + pair][:], SCORE_FACTOR, bg[:, rows, cols(h)], ALU.mult, ALU.add
+                )
+                nc.scalar.activation(th[:, rows, cols(h)], b_sum[:, rows, cols(h)], ACT.Tanh)
+
+        out_rows = out_0.rearrange("(p t) n -> p t n", t=R)
+        words_out = out_1[0].rearrange("p n t -> p (n t)").bitcast(I32)
+        out_w = tile("out_w", [P, S], U32)
+        out_s = tile("out_s", [P, S], U8)
+        for h in range(2):
+            for pair in range(2):
+                rows = slice(2 * pair, 2 * pair + 2)
+                nc.vector.scalar_tensor_tensor(
+                    res[:, rows, cols(h)], th[:, rows, cols(h)], 1.0, a_sum[:, rows, cols(h)], ALU.add, ALU.mult
                 )
                 nc.sync.dma_start(out_rows[:, rows, cols(h)], res[:, rows, cols(h)])
-            rounded = tile("o_r%d" % h, [P, R * HALF], BF16)
-            nc.vector.tensor_copy(woven(rounded), by_pairs(res, h))
-            nc.vector.quantize_mx(o_w[:, cols(h)].bitcast(FP8X4), o_s[:, cols(h)], rounded[:])
-            nc.sync.dma_start(words_out[:, cols(h)], o_w[:, cols(h)].bitcast(I32))
+            for quarter in (2 * h, 2 * h + 1):
+                part = slice(P * quarter, P * (quarter + 1))
+                rounded = tile("out_rounded%d" % quarter, [P, R * P], BF16)
+                if quarter < ROUNDED_ON_SCALAR:
+                    nc.scalar.copy(woven(rounded), in_pairs(res[:, :, part]))
+                else:
+                    nc.vector.tensor_copy(woven(rounded), in_pairs(res[:, :, part]))
+                nc.vector.quantize_mx(out_w[:, part].bitcast(FP8X4), out_s[:, part], rounded[:])
+            queue = nc.scalar if h == 1 else nc.sync
+            queue.dma_start(words_out[:, cols(h)], out_w[:, cols(h)].bitcast(I32))
         for q in range(4):
-            engine = nc.scalar if q % 2 else nc.sync
-            engine.dma_start(out_2[0, 4 * q : 4 * q + 4, :].bitcast(I32), o_s[32 * q : 32 * q + 4, :].bitcast(I32))
+            queue = nc.scalar if q % 2 else nc.sync
+            queue.dma_start(out_2[0, 4 * q : 4 * q + 4, :].bitcast(I32), out_s[32 * q : 32 * q + 4, :].bitcast(I32))

@@ -20,10 +20,10 @@ P = 128
 R = 4
 HALF = S // 2
 SCORE_FACTOR = 0.0625 * 0.5
+WORDS_AHEAD = 768
 
 SCALED_ON_GPSIMD = 2
 N3_ON_VECTOR = 3
-A_ON_VECTOR = 1
 N6_ON_VECTOR = 3
 ROUNDED_ON_SCALAR = 3
 EARLY_MIDDLES = 1
@@ -51,28 +51,29 @@ def tile_picked_twocdtriebhopmed_none_po_kernel(
             nc.sync.dma_start(dst[:], src)
             return dst
 
-        def load_scales(name, src, width):
-            dst = tile(name, [P, width], U8)
+        def load_scales(dst, src):
             for q in range(4):
-                rows = src[0, 4 * q : 4 * q + 4, :].bitcast(I32)
-                nc.sync.dma_start(
-                    dst[32 * q : 32 * (q + 1), :].bitcast(I32), rows.unsqueeze(0).broadcast_to([8, 4, width // 4])
-                )
-            return dst
+                nc.sync.dma_start(dst[32 * q : 32 * q + 4, :].bitcast(I32), src[0, 4 * q : 4 * q + 4, :].bitcast(I32))
 
         def load_factors(name, src):
             dst = tile(name, [P, R], F32)
             nc.sync.dma_start(dst[:], src.rearrange("(p t) o -> p (t o)", t=R))
             return dst
 
+        xs = tile("xs", [P, T], U8)
+        w1s = tile("w1s", [P, H], U8)
+        nc.gpsimd.memset(xs[:].bitcast(I32), 0)
+        nc.gpsimd.memset(w1s[:].bitcast(I32), 0)
+        xw = tile("xw", [P, T], I32)
+        xw_src = x_words[0].rearrange("p n t -> p (n t)").bitcast(I32)
+        w1w = tile("w1w", [P, 2 * H], U8)
         l_offs = load_list("offs", offs)
         l_ca = load_list("ca", ca)
-        xs = load_scales("xs", x_scales, T)
-        xw = tile("xw", [P, T], I32)
-        nc.sync.dma_start(xw[:], x_words[0].rearrange("p n t -> p (n t)").bitcast(I32))
-        w1w = tile("w1w", [P, 2 * H], U8)
+        nc.sync.dma_start(xw[:, :WORDS_AHEAD], xw_src[:, :WORDS_AHEAD])
+        load_scales(xs, x_scales)
+        nc.sync.dma_start(xw[:, WORDS_AHEAD:], xw_src[:, WORDS_AHEAD:])
         nc.sync.dma_start(w1w[:].bitcast(I32), w1_words[0].bitcast(I32))
-        w1s = load_scales("w1s", w1_scales, H)
+        load_scales(w1s, w1_scales)
         g1 = load_factors("g1", gs)
         l_n1 = load_list("n1", n1)
         g2 = load_factors("g2", gs2)
@@ -86,7 +87,7 @@ def tile_picked_twocdtriebhopmed_none_po_kernel(
         def dealt(ap):
             return ap.rearrange("p (t m) -> p m t", t=R)
 
-        def pick_dealt_scales(name, lst, after=None):
+        def pick_dealt_scales(name, lst, after):
             dst = tile(name, [P, C], U8, after)
             nc.vector.tensor_copy(dealt(dst[:]), xs[:].indirect(lst[:]))
             return dst
@@ -103,7 +104,6 @@ def tile_picked_twocdtriebhopmed_none_po_kernel(
         )
         xq_s = tile("xq_s", [P, S], U8)
         nc.vector.tensor_copy(xq_s[:], xs[:].indirect(l_offs[:]))
-        ca_s = pick_dealt_scales("ca_s", l_ca)
         xq_w = tile("xq_w", [P, S], U32)
         nc.vector.tensor_copy(xq_w[:], xw[:].bitcast(U32).indirect(l_offs[:]))
         w1s_dealt = tile("w1s_dealt", [P, H], U8)
@@ -186,7 +186,8 @@ def tile_picked_twocdtriebhopmed_none_po_kernel(
             else:
                 nc.gpsimd.tensor_tensor(st[:, t, :], ya[t][:], hop1[t][:], ALU.add)
         ca_w = pick_dealt_words("ca_w", l_ca, "w1s")
-        cb_s = pick_dealt_scales("cb_s", l_cb, "xq_s")
+        ca_s = pick_dealt_scales("ca_s", l_ca, "xq_s")
+        cb_s = pick_dealt_scales("cb_s", l_cb, "w1s_dealt")
         for t in range(SCALED_ON_GPSIMD, R):
             leave_psum(t < N3_ON_VECTOR, yb[t][:], y_ps[t][:], g2[:, t : t + 1])
         cb_w = pick_dealt_words("cb_w", l_cb, "xq_w")
@@ -219,15 +220,13 @@ def tile_picked_twocdtriebhopmed_none_po_kernel(
             for h in range(2):
                 score(a_ps[t][:, cols(h)], t, h, ca_w, ca_s, z_w, z_s)
         aw, ag, bw = (planes(n) for n in ("aw", "ag", "bw"))
-        for t in range(A_ON_VECTOR):
-            leave_psum(True, aw[t][:], a_ps[t][:], SCORE_FACTOR)
         for t in range(R):
             if t >= N3_ON_VECTOR:
                 bounds(t)
             if t >= EARLY_MIDDLES:
                 middle(t)
         z2_w, z2_s = quantise("z2", lo, mid, ALU.max)
-        for t in range(A_ON_VECTOR, R):
+        for t in range(R):
             leave_psum(False, aw[t][:], a_ps[t][:], SCORE_FACTOR)
 
         b_ps = [psum.tile([P, 2, HALF], F32, name="b%d" % u, tag="y_then_b%d" % u) for u in range(R)]

from contextlib import ExitStack

import concourse.mybir as mybir

K, T, S, H, C = 512, 2048, 512, 512, 512
FLOPS = 2 * K * H * S + 2 * (2 * H * C * S)

F32 = mybir.dt.float32
BF16 = mybir.dt.bfloat16
I32 = mybir.dt.int32
U32 = mybir.dt.uint32
U16 = mybir.dt.uint16
U8 = mybir.dt.uint8
FP8X4 = mybir.dt.float8_e4m3fn_x4
FP4X4 = mybir.dt.float4_e2m1fn_x4
ALU = mybir.AluOpType
ACT = mybir.ActivationFunctionType

P = 128
R = 4
HALF = S // 2
SCORE_FACTOR = 0.0625 * 0.5
WORDS_AHEAD = 768

SCALED_ON_GPSIMD = 2
N3_ON_VECTOR = 3
N6_ON_VECTOR = 3
ROUNDED_ON_SCALAR = 3
EARLY_MIDDLES = 1


def tile_picked_twocdtriebhopmed_none_po_kernel(
    tc, x_words, x_scales, w1_words, w1_scales, gs, gs2, offs, n1, n2, n3, n4, ca, cb, n5, n6, out_0, out_1, out_2
):
    nc = tc.nc
    with ExitStack() as ctx:
        sbuf = ctx.enter_context(tc.tile_pool(name="sbuf", bufs=1))
        psum = ctx.enter_context(tc.psum_pool(name="psum", bufs=1))

        def tile(name, shape, dtype, after=None):
            return sbuf.tile(shape, dtype, name=name, tag=after or name, align_bytes=64)

        def planes(name):
            return [tile("%s%d" % (name, t), [P, S], F32) for t in range(R)]

        def cols(h):
            return slice(HALF * h, HALF * (h + 1))

        def load_list(name, src):
            dst = tile("list_" + name, [P, S // 16], U16)
            nc.sync.dma_start(dst[:], src)
            return dst

        def load_scales(dst, src):
            for q in range(4):
                nc.sync.dma_start(dst[32 * q : 32 * q + 4, :].bitcast(I32), src[0, 4 * q : 4 * q + 4, :].bitcast(I32))

        def load_factors(name, src):
            dst = tile(name, [P, R], F32)
            nc.sync.dma_start(dst[:], src.rearrange("(p t) o -> p (t o)", t=R))
            return dst

        xs = tile("xs", [P, T], U8)
        w1s = tile("w1s", [P, H], U8)
        nc.gpsimd.memset(xs[:].bitcast(I32), 0)
        nc.gpsimd.memset(w1s[:].bitcast(I32), 0)
        xw = tile("xw", [P, T], I32)
        xw_src = x_words[0].rearrange("p n t -> p (n t)").bitcast(I32)
        w1w = tile("w1w", [P, 2 * H], U8)
        l_offs = load_list("offs", offs)
        l_ca = load_list("ca", ca)
        nc.sync.dma_start(xw[:, :WORDS_AHEAD], xw_src[:, :WORDS_AHEAD])
        load_scales(xs, x_scales)
        nc.sync.dma_start(xw[:, WORDS_AHEAD:], xw_src[:, WORDS_AHEAD:])
        nc.sync.dma_start(w1w[:].bitcast(I32), w1_words[0].bitcast(I32))
        load_scales(w1s, w1_scales)
        g1 = load_factors("g1", gs)
        l_n1 = load_list("n1", n1)
        g2 = load_factors("g2", gs2)
        l_n2 = load_list("n2", n2)
        l_cb = load_list("cb", cb)
        l_n4 = load_list("n4", n4)
        l_n3 = load_list("n3", n3)
        l_n5 = load_list("n5", n5)
        l_n6 = load_list("n6", n6)

        def dealt(ap):
            return ap.rearrange("p (t m) -> p m t", t=R)

        def pick_dealt_scales(name, lst, after):
            dst = tile(name, [P, C], U8, after)
            nc.vector.tensor_copy(dealt(dst[:]), xs[:].indirect(lst[:]))
            return dst

        def pick_dealt_words(name, lst, after):
            dst = tile(name, [P, C], U32, after)
            nc.vector.tensor_copy(dealt(dst[:]), xw[:].bitcast(U32).indirect(lst[:]))
            return dst

        w1w_dealt = tile("w1w_dealt", [P, 2 * H], U8)
        nc.scalar.copy(
            w1w_dealt[:].bitcast(U16).rearrange("p (t m) -> p t m", t=R),
            w1w[:].bitcast(U16).rearrange("p (m t) -> p t m", t=R),
        )
        xq_s = tile("xq_s", [P, S], U8)
        nc.vector.tensor_copy(xq_s[:], xs[:].indirect(l_offs[:]))
        xq_w = tile("xq_w", [P, S], U32)
        nc.vector.tensor_copy(xq_w[:], xw[:].bitcast(U32).indirect(l_offs[:]))
        w1s_dealt = tile("w1s_dealt", [P, H], U8)
        nc.vector.tensor_copy(
            w1s_dealt[:].rearrange("p (t m) -> p t m", t=R), w1s[:].rearrange("p (m t) -> p t m", t=R)
        )

        y_ps = [psum.tile([P, S], F32, name="y%d" % t, tag="y_then_b%d" % t) for t in range(R)]
        for t in range(R):
            nc.tensor.matmul_mx(
                out=y_ps[t][:],
                lhsT=w1w_dealt[:, 2 * P * t : 2 * P * (t + 1)].bitcast(FP4X4),
                lhsT_scale=w1s_dealt[:, P * t : P * (t + 1)],
                rhs=xq_w[:].bitcast(FP8X4),
                rhs_scale=xq_s[:],
                start=True,
                stop=True,
            )

        def leave_psum(on_vector, dst, bank, factor):
            if on_vector:
                nc.vector.tensor_scalar(dst, bank, factor, None, ALU.mult)
            else:
                nc.scalar.activation(dst, bank, ACT.Copy, scale=factor)

        def fetch_half(on_vector, dst, window, lst, h, factor=1.0):
            src = window.indirect(lst[:, HALF // 16 * h : HALF // 16 * (h + 1)])
            if on_vector:
                nc.vector.tensor_copy(dst[:, cols(h)], src)
            else:
                nc.scalar.activation(dst[:, cols(h)], src, ACT.Copy, scale=factor)

        def fetch(on_vector, dst, window, lst, factor=1.0):
            for h in range(2):
                fetch_half(on_vector, dst, window, lst, h, factor)

        def scale_on_gpsimd(dst, src, factor):
            nc.gpsimd.tensor_scalar(dst, src, factor, 0.0, ALU.mult, ALU.add)

        def in_pairs(src):
            return src.rearrange("p t (c i) -> p c t i", i=2)

        def woven(dst):
            return dst[:].rearrange("p (c i t) -> p c t i", i=2, t=R)

        def quantise(name, left, right, op):
            words = tile(name + "_w", [P, S], U32)
            scales = tile(name + "_s", [P, S], U8)
            for h in range(2):
                rounded = tile("%s_rounded%d" % (name, h), [P, R * HALF], BF16)
                nc.vector.tensor_tensor(woven(rounded), in_pairs(left[:, :, cols(h)]), in_pairs(right[:, :, cols(h)]), op)
                nc.vector.quantize_mx(words[:, cols(h)].bitcast(FP8X4), scales[:, cols(h)], rounded[:])
            return words, scales

        def score(out, t, h, picked_w, picked_s, words, scales):
            nc.tensor.matmul_mx(
                out=out,
                lhsT=picked_w[:, P * t : P * (t + 1)].bitcast(FP8X4),
                lhsT_scale=picked_s[:, P * t : P * (t + 1)],
                rhs=words[:, cols(h)].bitcast(FP8X4),
                rhs_scale=scales[:, cols(h)],
                start=True,
                stop=True,
            )

        ya, yb, hop1, pa, pb, hi = (planes(n) for n in ("ya", "yb", "hop1_", "pa", "pb", "hi"))
        unscaled_st = tile("unscaled_st", [P, R, S], F32)
        st = tile("st", [P, R, S], F32)
        hop2 = tile("hop2", [P, R, S], F32)
        lo = tile("lo", [P, R, S], F32)
        for t in range(R):
            leave_psum(t > 0, ya[t][:], y_ps[t][:], 1.0 if t < SCALED_ON_GPSIMD else g1[:, t : t + 1])
            fetch(False, hop1[t], ya[t][:], l_n1, 0.5)
        for t in range(SCALED_ON_GPSIMD):
            scale_on_gpsimd(yb[t][:], ya[t][:], g2[:, t : t + 1])
        for t in range(R):
            if t < SCALED_ON_GPSIMD:
                nc.gpsimd.tensor_tensor(unscaled_st[:, t, :], ya[t][:], hop1[t][:], ALU.add)
                scale_on_gpsimd(st[:, t, :], unscaled_st[:, t, :], g1[:, t : t + 1])
            else:
                nc.gpsimd.tensor_tensor(st[:, t, :], ya[t][:], hop1[t][:], ALU.add)
        ca_w = pick_dealt_words("ca_w", l_ca, "w1s")
        ca_s = pick_dealt_scales("ca_s", l_ca, "xq_s")
        cb_s = pick_dealt_scales("cb_s", l_cb, "w1s_dealt")
        for t in range(SCALED_ON_GPSIMD, R):
            leave_psum(t < N3_ON_VECTOR, yb[t][:], y_ps[t][:], g2[:, t : t + 1])
        cb_w = pick_dealt_words("cb_w", l_cb, "xq_w")
        for t in range(R):
            fetch(False, hop2[:, t, :], st[:, t, :], l_n2)

        for t in range(R):
            if t >= N3_ON_VECTOR:
                fetch(False, pa[t], yb[t][:], l_n3)
            fetch(False, pb[t], yb[t][:], l_n4)
        for t in range(N3_ON_VECTOR):
            fetch(True, pa[t], yb[t][:], l_n3)
        mid = tile("mid", [P, R, S], F32, "unscaled_st")

        def bounds(t):
            nc.vector.scalar_tensor_tensor(hi[t][:], y_ps[t][:], g2[:, t : t + 1], pa[t][:], ALU.mult, ALU.max)
            nc.vector.scalar_tensor_tensor(lo[:, t, :], y_ps[t][:], g2[:, t : t + 1], pa[t][:], ALU.mult, ALU.min)

        def middle(t):
            nc.vector.tensor_tensor(mid[:, t, :], hi[t][:], pb[t][:], ALU.min)

        for t in range(N3_ON_VECTOR):
            bounds(t)
        for t in range(EARLY_MIDDLES):
            middle(t)

        z_w, z_s = quantise("z", st, hop2, ALU.subtract)
        a_ps = [psum.tile([P, S], F32, name="a%d" % t) for t in range(R)]
        for t in range(R):
            for h in range(2):
                score(a_ps[t][:, cols(h)], t, h, ca_w, ca_s, z_w, z_s)
        aw, ag, bw = (planes(n) for n in ("aw", "ag", "bw"))
        for t in range(R):
            if t >= N3_ON_VECTOR:
                bounds(t)
            if t >= EARLY_MIDDLES:
                middle(t)
        z2_w, z2_s = quantise("z2", lo, mid, ALU.max)
        for t in range(R):
            leave_psum(False, aw[t][:], a_ps[t][:], SCORE_FACTOR)

        b_ps = [psum.tile([P, 2, HALF], F32, name="b%d" % u, tag="y_then_b%d" % u) for u in range(R)]
        for h in range(2):
            for t in range(R):
                score(b_ps[2 * h + t // 2][:, t % 2, :], t, h, cb_w, cb_s, z2_w, z2_s)
        for h in range(2):
            for t in range(R):
                leave_psum(True, bw[t][:, cols(h)], b_ps[2 * h + t // 2][:, t % 2, :], SCORE_FACTOR)
        for t in range(R):
            fetch(False, ag[t], aw[t][:], l_n5)

        a_sum = tile("a_sum", [P, R, S], F32, "z2_rounded1")
        for h in range(2):
            for t in range(R):
                nc.gpsimd.tensor_tensor(a_sum[:, t, cols(h)], aw[t][:, cols(h)], ag[t][:, cols(h)], ALU.add)

        bg = tile("bg", [P, R, S], F32)
        b_sum = tile("b_sum", [P, R, S], F32)
        th = tile("th", [P, R, S], F32)
        res = tile("res", [P, R, S], F32)
        for h in range(2):
            for pair in range(2):
                rows = slice(2 * pair, 2 * pair + 2)
                for t in (2 * pair, 2 * pair + 1):
                    fetch_half(R * h + t < N6_ON_VECTOR, bg[:, t, :], bw[t][:], l_n6, h)
                nc.vector.scalar_tensor_tensor(
                    b_sum[:, rows, cols(h)], b_ps[2 * h + pair][:], SCORE_FACTOR, bg[:, rows, cols(h)], ALU.mult, ALU.add
                )
                nc.scalar.activation(th[:, rows, cols(h)], b_sum[:, rows, cols(h)], ACT.Tanh)

        out_rows = out_0.rearrange("(p t) n -> p t n", t=R)
        words_out = out_1[0].rearrange("p n t -> p (n t)").bitcast(I32)
        out_w = tile("out_w", [P, S], U32)
        out_s = tile("out_s", [P, S], U8)
        for h in range(2):
            for pair in range(2):
                rows = slice(2 * pair, 2 * pair + 2)
                nc.vector.scalar_tensor_tensor(
                    res[:, rows, cols(h)], th[:, rows, cols(h)], 1.0, a_sum[:, rows, cols(h)], ALU.add, ALU.mult
                )
                nc.sync.dma_start(out_rows[:, rows, cols(h)], res[:, rows, cols(h)])
            for quarter in (2 * h, 2 * h + 1):
                part = slice(P * quarter, P * (quarter + 1))
                rounded = tile("out_rounded%d" % quarter, [P, R * P], BF16)
                if quarter < ROUNDED_ON_SCALAR:
                    nc.scalar.copy(woven(rounded), in_pairs(res[:, :, part]))
                else:
                    nc.vector.tensor_copy(woven(rounded), in_pairs(res[:, :, part]))
                nc.vector.quantize_mx(out_w[:, part].bitcast(FP8X4), out_s[:, part], rounded[:])
            queue = nc.scalar if h == 1 else nc.sync
            queue.dma_start(words_out[:, cols(h)], out_w[:, cols(h)].bitcast(I32))
        for q in range(4):
            queue = nc.scalar if q % 2 else nc.sync
            queue.dma_start(out_2[0, 4 * q : 4 * q + 4, :].bitcast(I32), out_s[32 * q : 32 * q + 4, :].bitcast(I32))
